import numpy as np, ml_dtypes
CORES = [88,96,104,112,120,216,224,232,240,248]
N = 10
C = 64
def setup_inputs(rng):
    x = rng.standard_normal((N, 128, C), dtype=np.float32) * (0.25 + np.abs(rng.standard_normal((N, 1, C), dtype=np.float32)))
    return {"x": x.astype(ml_dtypes.bfloat16)}
def setup_inputs_big(rng):
    d = setup_inputs(rng)
    for k in ("x",): d[k] = (d[k].astype(np.float32) * 1048576.0).astype(d[k].dtype)
    return d
def setup_inputs_small(rng):
    d = setup_inputs(rng)
    for k in ("x",): d[k] = (d[k].astype(np.float32) * (1 / 1048576.0)).astype(d[k].dtype)
    return d
def setup_inputs_apart(rng):
    d = setup_inputs(rng)
    f = (10.0 ** rng.permutation(np.linspace(-1.5, 1.5, N))).astype(np.float32).reshape(N, 1, 1)
    for k in ("x",): d[k] = (d[k].astype(np.float32) * f).astype(d[k].dtype)
    return d
def setup_inputs_mixed(rng):
    d = setup_inputs(rng)
    f = (10.0 ** rng.uniform(-3, 3, (N, 1, C))).astype(np.float32); shape = rng.integers(3, size=(N, 1, C))
    for k in ("x",):
        x = d[k].astype(np.float32)
        m = x.mean(axis=1, keepdims=True); level = m + np.sign(x - m) * np.abs(x - m).mean(axis=1, keepdims=True) * rng.uniform(0.9, 1.1, x.shape).astype(np.float32)
        other = x * np.where(rng.random(x.shape) < 0.016, 100.0, 1.0).astype(np.float32)
        d[k] = (np.where(shape == 1, level, np.where(shape == 2, other, x)) * f).astype(d[k].dtype)
    return d
def reference(x):
    X = x.astype(np.float64); U = X / np.sqrt((X ** 2).sum(axis=1, keepdims=True))
    y = np.full((N, C, N * C), np.nan)
    for r in range(N):
        for s in range(N):
            if s != r: y[r][:, C * s:C * s + C] = U[r].T @ U[s]
    return {"y": y.astype(ml_dtypes.bfloat16)}

@@ -1,0 +1,182 @@
+from concourse.bass import DstId, RemoteDMATransfer
+from concourse.mybir import AluOpType, ActivationFunctionType
+
+NSIM = 256
+C = 64
+NR = 10
+NBANK = 8
+ENG_CHIP = 8
+ENG_OUT = 8
+NRELAY = 2
+
+SCRATCH = {
+    "xs": ("sbuf", [128, C], "bfloat16"),
+    "sq": ("sbuf", [128, C], "bfloat16"),
+    "ones": ("sbuf", [128, 128], "bfloat16"),
+    "rs": ("sbuf", [128, C], "float32"),
+    "inv": ("sbuf", [128, C], "bfloat16"),
+    "u": ("sbuf", [128, C], "bfloat16"),
+    "land": ("sbuf", [128, NR * C], "bfloat16"),
+    "yb": ("sbuf", [128, NR * C], "bfloat16"),
+}
+for _b in range(NBANK):
+    SCRATCH["ps%d" % _b] = ("psum", [128, 512], "float32")
+
+SEMAPHORES = (["ld", "cst", "c1", "c2", "c3", "c4", "c5", "h", "ae", "e0", "e1", "cp", "loc", "st"]
+              + ["a%d" % _s for _s in range(NR)] + ["m%d" % _s for _s in range(NR)])
+
+
+def _take(mask, n):
+    out, bit = 0, 1
+    while n > 0 and bit <= mask:
+        if mask & bit:
+            out |= bit
+            n -= 1
+        bit <<= 1
+    return out
+
+
+def _count(mask):
+    n = 0
+    while mask:
+        n += mask & 1
+        mask >>= 1
+    return n
+
+
+def _plan(T, topo):
+    cores = list(T.cores)
+    plan = {}
+    for c in cores:
+        group = [d for d in cores if d == c or topo.may_write(c, d)]
+        cross = [d for d in cores if d not in group]
+        q = group.index(c)
+        direct = group[q + 1:] + group[:q]
+        here = [h for h in range(NSIM) if h not in cores
+                and topo.host(h) == topo.host(c) and topo.chip(h) == topo.chip(c)]
+        owners = [h for h in here if all(topo.may_write(h, d) for d in cross)]
+        dies = sorted(set(topo.die(h) for h in owners), key=lambda v: v != topo.die(c))
+        relays = [[h for h in owners if topo.die(h) == v][0] for v in dies][:NRELAY]
+        k = len(relays)
+        shares = []
+        for j in range(k):
+            part = [cross[p] for p in range(len(cross)) if (p + q) % k == j]
+            rot = (q // k) % len(part)
+            shares.append(part[rot:] + part[:rot])
+        plan[c] = {"direct": direct, "relays": relays, "shares": shares}
+    return plan
+
+
+def _fused(g, topo, core, dsts, mask, sem, src, dst, local_sem):
+    ids = []
+    for d in dsts:
+        rid, pid = topo.addr(d, core)
+        ids.append(DstId(rid=rid, pnc=pid))
+    g.remote_dma_fused([RemoteDMATransfer(dst_ids=ids, dma_engine_mask=mask, remote_sem=sem,
+                                          srcs=[src], dsts=[dst for _ in dsts], alu_op=0)], local_sem=local_sem)
+
+
+def _common_mask(topo, core, dsts):
+    m = topo.mask(core, dsts[0])
+    for d in dsts:
+        m &= topo.mask(core, d)
+    return m
+
+
+def rank_program(g, core, T, topo):
+    S = T.sem
+    plan = _plan(T, topo)
+    cores = list(T.cores)
+    rank = T.rank_of(core)
+
+    if rank is None:
+        for c in cores:
+            if core in plan[c]["relays"]:
+                s = T.rank_of(c)
+                dsts = plan[c]["shares"][plan[c]["relays"].index(core)]
+                n_in = _count(_take(_common_mask(topo, c, plan[c]["relays"] + plan[c]["direct"]), ENG_CHIP))
+                g.vector.wait_ge(S.h, 2 * n_in)
+                g.vector.tensor_tensor(T.u[:], T.xs[:], T.inv[:], AluOpType.mult).then_inc(S.c5, 1)
+                m = _take(_common_mask(topo, core, dsts), ENG_OUT)
+                g.wait_ge(S.c5, 1)
+                _fused(g, topo, core, dsts, m, S["a%d" % s], T.u[:], T.land[:, s * C:(s + 1) * C], S.loc)
+                g.wait_ge(S.loc, _count(m))
+        return
+
+    me = plan[core]
+    direct, relays = me["direct"], me["relays"]
+    m_chip = _take(_common_mask(topo, core, relays + direct), ENG_CHIP)
+    m_out = _take(_common_mask(topo, core, direct), ENG_OUT)
+
+    early = [T.rank_of(c) for c in cores if core in plan[c]["direct"]]
+    late = []
+    for c in cores:
+        for relay, share in zip(plan[c]["relays"], plan[c]["shares"]):
+            if core in share:
+                late.append((share.index(core), T.rank_of(c), _count(_take(_common_mask(topo, relay, share), ENG_OUT))))
+    late.sort()
+    n_early = 0
+    for c in cores:
+        if core in plan[c]["direct"]:
+            n_early += _count(_take(_common_mask(topo, c, plan[c]["direct"]), ENG_OUT))
+
+    g.sync.dma_start(T.xs[:], T.x[:]).then_inc(S.ld, 16)
+    g.vector.memset(T.ones[:], 1.0).then_inc(S.cst, 1)
+    g.vector.memset(T.yb[0:C, rank * C:(rank + 1) * C], 0.0).then_inc(S.cp, 1)
+
+    g.wait_ge(S.ld, 16)
+    _fused(g, topo, core, relays, m_chip, S.h, T.xs[:], T.xs[:], S.loc)
+
+    g.scalar.wait_ge(S.ld, 16)
+    g.scalar.activation(T.sq[:], T.xs[:], ActivationFunctionType.Square).then_inc(S.c1, 1)
+    g.tensor.wait_ge(S.cst, 1)
+    g.tensor.wait_ge(S.c1, 1)
+    g.tensor.matmul(T.ps0[:, 0:C], T.ones[:], T.sq[:], True, True).then_inc(S.c2, 1)
+    g.vector.wait_ge(S.c2, 1)
+    g.vector.reciprocal(T.rs[:], T.ps0[:, 0:C]).then_inc(S.c3, 1)
+    g.scalar.wait_ge(S.c3, 1)
+    g.scalar.activation(T.inv[:], T.rs[:], ActivationFunctionType.Sqrt).then_inc(S.c4, 1)
+
+    g.wait_ge(S.c4, 1)
+    _fused(g, topo, core, relays, m_chip, S.h, T.inv[:], T.inv[:], S.loc)
+
+    g.vector.wait_ge(S.c4, 1)
+    g.vector.tensor_tensor(T.u[:], T.xs[:], T.inv[:], AluOpType.mult).then_inc(S.c5, 1)
+    g.wait_ge(S.c5, 1)
+    _fused(g, topo, core, direct, m_out, S.ae, T.u[:], T.land[:, rank * C:(rank + 1) * C], S.loc)
+
+    banks = ["ps%d" % b for b in range(1, NBANK)]
+    late_bank = banks[:len(late)]
+    early_bank = banks[len(late):][:2]
+    copiers = [g.vector, g.scalar]
+
+    def copy(which, out, in_):
+        if which == 0:
+            return g.vector.tensor_copy(out, in_)
+        return g.scalar.activation(out, in_, ActivationFunctionType.Copy)
+
+    g.tensor.wait_ge(S.c5, 1)
+    g.tensor.wait_ge(S.ae, n_early)
+    per_bank = [[] for _ in early_bank]
+    for i, s in enumerate(early):
+        per_bank[i % len(early_bank)].append(s)
+    for b, blocks in enumerate(per_bank):
+        for i, s in enumerate(blocks):
+            g.tensor.matmul(T[early_bank[b]][0:C, i * C:(i + 1) * C], T.u[:], T.land[:, s * C:(s + 1) * C],
+                            True, True).then_inc(S["e%d" % b], 1)
+    for b, blocks in enumerate(per_bank):
+        copiers[b % 2].wait_ge(S["e%d" % b], len(blocks))
+        for i, s in enumerate(blocks):
+            copy(b % 2, T.yb[0:C, s * C:(s + 1) * C], T[early_bank[b]][0:C, i * C:(i + 1) * C]).then_inc(S.cp, 1)
+
+    for i, (pos, s, n) in enumerate(late):
+        g.tensor.wait_ge(S["a%d" % s], n)
+        g.tensor.matmul(T[late_bank[i]][0:C, 0:C], T.u[:], T.land[:, s * C:(s + 1) * C],
+                        True, True).then_inc(S["m%d" % s], 1)
+        copiers[i % 2].wait_ge(S["m%d" % s], 1)
+        copy(i % 2, T.yb[0:C, s * C:(s + 1) * C], T[late_bank[i]][0:C, 0:C]).then_inc(S.cp, 1)
+
+    g.sync.wait_ge(S.cp, NR)
+    g.sync.dma_start(T.y[:], T.yb[0:C, :]).then_inc(S.st, 16)
+    g.sync.wait_ge(S.st, 16)
+    g.wait_ge(S.loc, 2 * _count(m_chip) + _count(m_out))

@@ -3,6 +3,7 @@ from concourse.mybir import AluOpType, ActivationFunctionType
 
 NSIM = 256
 C = 64
+W = 2 * C
 NR = 10
 NBANK = 8
 ENG_CHIP = 8
@@ -10,20 +11,21 @@ ENG_OUT = 8
 NRELAY = 2
 
 SCRATCH = {
-    "xs": ("sbuf", [128, C], "bfloat16"),
+    "msg": ("sbuf", [128, W], "bfloat16"),
     "sq": ("sbuf", [128, C], "bfloat16"),
     "ones": ("sbuf", [128, 128], "bfloat16"),
     "rs": ("sbuf", [128, C], "float32"),
     "inv": ("sbuf", [128, C], "bfloat16"),
     "u": ("sbuf", [128, C], "bfloat16"),
-    "land": ("sbuf", [128, NR * C], "bfloat16"),
+    "land": ("sbuf", [128, NR * W], "bfloat16"),
+    "iv": ("sbuf", [128, NR * C], "float32"),
     "yb": ("sbuf", [128, NR * C], "bfloat16"),
 }
 for _b in range(NBANK):
     SCRATCH["ps%d" % _b] = ("psum", [128, 512], "float32")
 
-SEMAPHORES = (["ld", "cst", "c1", "c2", "c3", "c4", "c5", "h", "ae", "e0", "e1", "cp", "loc", "st"]
-              + ["a%d" % _s for _s in range(NR)] + ["m%d" % _s for _s in range(NR)])
+SEMAPHORES = (["ld", "cst", "c1", "c2", "c3", "c4", "c5", "c6", "h", "ae", "e0", "ev", "cp", "loc", "st"]
+              + ["a%d" % _s for _s in range(NR)] + ["m%d" % _s for _s in range(NR)] + ["v%d" % _s for _s in range(NR)])
 
 
 def _take(mask, n):
@@ -88,6 +90,7 @@ def rank_program(g, core, T, topo):
     plan = _plan(T, topo)
     cores = list(T.cores)
     rank = T.rank_of(core)
+    Act = ActivationFunctionType
 
     if rank is None:
         for c in cores:
@@ -95,11 +98,9 @@ def rank_program(g, core, T, topo):
                 s = T.rank_of(c)
                 dsts = plan[c]["shares"][plan[c]["relays"].index(core)]
                 n_in = _count(_take(_common_mask(topo, c, plan[c]["relays"] + plan[c]["direct"]), ENG_CHIP))
-                g.vector.wait_ge(S.h, 2 * n_in)
-                g.vector.tensor_tensor(T.u[:], T.xs[:], T.inv[:], AluOpType.mult).then_inc(S.c5, 1)
                 m = _take(_common_mask(topo, core, dsts), ENG_OUT)
-                g.wait_ge(S.c5, 1)
-                _fused(g, topo, core, dsts, m, S["a%d" % s], T.u[:], T.land[:, s * C:(s + 1) * C], S.loc)
+                g.wait_ge(S.h, 2 * n_in)
+                _fused(g, topo, core, dsts, m, S["a%d" % s], T.msg[:], T.land[:, s * W:(s + 1) * W], S.loc)
                 g.wait_ge(S.loc, _count(m))
         return
 
@@ -120,61 +121,67 @@ def rank_program(g, core, T, topo):
         if core in plan[c]["direct"]:
             n_early += _count(_take(_common_mask(topo, c, plan[c]["direct"]), ENG_OUT))
 
-    g.sync.dma_start(T.xs[:], T.x[:]).then_inc(S.ld, 16)
+    x = T.msg[:, 0:C]
+    q = T.msg[:, C:W]
+
+    g.sync.dma_start(x, T.x[:]).then_inc(S.ld, 16)
     g.vector.memset(T.ones[:], 1.0).then_inc(S.cst, 1)
     g.vector.memset(T.yb[0:C, rank * C:(rank + 1) * C], 0.0).then_inc(S.cp, 1)
 
     g.wait_ge(S.ld, 16)
-    _fused(g, topo, core, relays, m_chip, S.h, T.xs[:], T.xs[:], S.loc)
+    _fused(g, topo, core, relays, m_chip, S.h, x, x, S.loc)
 
     g.scalar.wait_ge(S.ld, 16)
-    g.scalar.activation(T.sq[:], T.xs[:], ActivationFunctionType.Square).then_inc(S.c1, 1)
+    g.scalar.activation(T.sq[:], x, Act.Square).then_inc(S.c1, 1)
     g.tensor.wait_ge(S.cst, 1)
     g.tensor.wait_ge(S.c1, 1)
     g.tensor.matmul(T.ps0[:, 0:C], T.ones[:], T.sq[:], True, True).then_inc(S.c2, 1)
     g.vector.wait_ge(S.c2, 1)
     g.vector.reciprocal(T.rs[:], T.ps0[:, 0:C]).then_inc(S.c3, 1)
-    g.scalar.wait_ge(S.c3, 1)
-    g.scalar.activation(T.inv[:], T.rs[:], ActivationFunctionType.Sqrt).then_inc(S.c4, 1)
+    g.vector.wait_ge(S.c3, 1)
+    g.vector.tensor_copy(q, T.rs[:]).then_inc(S.c4, 1)
 
     g.wait_ge(S.c4, 1)
-    _fused(g, topo, core, relays, m_chip, S.h, T.inv[:], T.inv[:], S.loc)
+    _fused(g, topo, core, relays, m_chip, S.h, q, q, S.loc)
+    _fused(g, topo, core, direct, m_out, S.ae, T.msg[:], T.land[:, rank * W:(rank + 1) * W], S.loc)
 
-    g.vector.wait_ge(S.c4, 1)
-    g.vector.tensor_tensor(T.u[:], T.xs[:], T.inv[:], AluOpType.mult).then_inc(S.c5, 1)
-    g.wait_ge(S.c5, 1)
-    _fused(g, topo, core, direct, m_out, S.ae, T.u[:], T.land[:, rank * C:(rank + 1) * C], S.loc)
+    g.scalar.wait_ge(S.c3, 1)
+    g.scalar.activation(T.inv[:], T.rs[:], Act.Sqrt).then_inc(S.c6, 1)
+    g.vector.wait_ge(S.c6, 1)
+    g.vector.tensor_tensor(T.u[:], x, T.inv[:], AluOpType.mult).then_inc(S.c5, 1)
 
     banks = ["ps%d" % b for b in range(1, NBANK)]
     late_bank = banks[:len(late)]
-    early_bank = banks[len(late):][:2]
-    copiers = [g.vector, g.scalar]
+    early_bank = banks[len(late)]
 
-    def copy(which, out, in_):
-        if which == 0:
-            return g.vector.tensor_copy(out, in_)
-        return g.scalar.activation(out, in_, ActivationFunctionType.Copy)
+    def xs(s):
+        return T.land[:, s * W:s * W + C]
+
+    def qs(s):
+        return T.land[0:C, s * W + C:(s + 1) * W]
+
+    def blk(t, s):
+        return t[0:C, s * C:(s + 1) * C]
 
     g.tensor.wait_ge(S.c5, 1)
     g.tensor.wait_ge(S.ae, n_early)
-    per_bank = [[] for _ in early_bank]
+    g.scalar.wait_ge(S.ae, n_early)
     for i, s in enumerate(early):
-        per_bank[i % len(early_bank)].append(s)
-    for b, blocks in enumerate(per_bank):
-        for i, s in enumerate(blocks):
-            g.tensor.matmul(T[early_bank[b]][0:C, i * C:(i + 1) * C], T.u[:], T.land[:, s * C:(s + 1) * C],
-                            True, True).then_inc(S["e%d" % b], 1)
-    for b, blocks in enumerate(per_bank):
-        copiers[b % 2].wait_ge(S["e%d" % b], len(blocks))
-        for i, s in enumerate(blocks):
-            copy(b % 2, T.yb[0:C, s * C:(s + 1) * C], T[early_bank[b]][0:C, i * C:(i + 1) * C]).then_inc(S.cp, 1)
+        g.tensor.matmul(blk(T[early_bank], i), T.u[:], xs(s), True, True).then_inc(S.e0, 1)
+        g.scalar.activation(blk(T.iv, s), qs(s), Act.Sqrt).then_inc(S.ev, 1)
+    g.vector.wait_ge(S.e0, len(early))
+    g.vector.wait_ge(S.ev, len(early))
+    for i, s in enumerate(early):
+        g.vector.tensor_tensor(blk(T.yb, s), blk(T[early_bank], i), blk(T.iv, s), AluOpType.mult).then_inc(S.cp, 1)
 
     for i, (pos, s, n) in enumerate(late):
         g.tensor.wait_ge(S["a%d" % s], n)
-        g.tensor.matmul(T[late_bank[i]][0:C, 0:C], T.u[:], T.land[:, s * C:(s + 1) * C],
-                        True, True).then_inc(S["m%d" % s], 1)
-        copiers[i % 2].wait_ge(S["m%d" % s], 1)
-        copy(i % 2, T.yb[0:C, s * C:(s + 1) * C], T[late_bank[i]][0:C, 0:C]).then_inc(S.cp, 1)
+        g.tensor.matmul(T[late_bank[i]][0:C, 0:C], T.u[:], xs(s), True, True).then_inc(S["m%d" % s], 1)
+        g.scalar.wait_ge(S["a%d" % s], n)
+        g.scalar.activation(blk(T.iv, s), qs(s), Act.Sqrt).then_inc(S["v%d" % s], 1)
+        g.vector.wait_ge(S["m%d" % s], 1)
+        g.vector.wait_ge(S["v%d" % s], 1)
+        g.vector.tensor_tensor(blk(T.yb, s), T[late_bank[i]][0:C, 0:C], blk(T.iv, s), AluOpType.mult).then_inc(S.cp, 1)
 
     g.sync.wait_ge(S.cp, NR)
     g.sync.dma_start(T.y[:], T.yb[0:C, :]).then_inc(S.st, 16)

@@ -3,29 +3,31 @@ from concourse.mybir import AluOpType, ActivationFunctionType
 
 NSIM = 256
 C = 64
-W = 2 * C
 NR = 10
-NBANK = 8
-ENG_CHIP = 8
-ENG_OUT = 8
-NRELAY = 2
+QP = 4
+ND = 3
+NH = 3
+ENG = 8
 
 SCRATCH = {
-    "msg": ("sbuf", [128, W], "bfloat16"),
+    "xm": ("sbuf", [128, C], "bfloat16"),
+    "qm": ("sbuf", [128, 1], "float32"),
     "sq": ("sbuf", [128, C], "bfloat16"),
-    "ones": ("sbuf", [128, 128], "bfloat16"),
-    "rs": ("sbuf", [128, C], "float32"),
-    "inv": ("sbuf", [128, C], "bfloat16"),
-    "u": ("sbuf", [128, C], "bfloat16"),
-    "land": ("sbuf", [128, NR * W], "bfloat16"),
-    "iv": ("sbuf", [128, NR * C], "float32"),
+    "one1": ("sbuf", [128, 1], "bfloat16"),
+    "ones": ("sbuf", [128, C], "bfloat16"),
+    "ident": ("sbuf", [128, C], "bfloat16"),
+    "ivc": ("sbuf", [128, 1], "float32"),
+    "land": ("sbuf", [128, NR * C], "bfloat16"),
+    "ql": ("sbuf", [128, NR * QP], "float32"),
+    "dg": ("sbuf", [128, NR * C], "bfloat16"),
+    "gs": ("sbuf", [128, NR * C], "float32"),
     "yb": ("sbuf", [128, NR * C], "bfloat16"),
 }
-for _b in range(NBANK):
+for _b in range(8):
     SCRATCH["ps%d" % _b] = ("psum", [128, 512], "float32")
 
-SEMAPHORES = (["ld", "cst", "c1", "c2", "c3", "c4", "c5", "c6", "h", "ae", "e0", "ev", "cp", "loc", "st"]
-              + ["a%d" % _s for _s in range(NR)] + ["m%d" % _s for _s in range(NR)] + ["v%d" % _s for _s in range(NR)])
+SEMAPHORES = (["ld", "cst", "idn", "c1", "c2", "c3", "c6", "hx", "hq", "e0", "eg", "er", "cp", "loc", "st"]
+              + [p + "%d" % _s for _s in range(NR) for p in ("ax", "aq", "mg", "cg", "dd", "rr")])
 
 
 def _take(mask, n):
@@ -46,6 +48,13 @@ def _count(mask):
     return n
 
 
+def _common_mask(topo, core, dsts):
+    m = topo.mask(core, dsts[0])
+    for d in dsts:
+        m &= topo.mask(core, d)
+    return m
+
+
 def _plan(T, topo):
     cores = list(T.cores)
     plan = {}
@@ -53,19 +62,24 @@ def _plan(T, topo):
         group = [d for d in cores if d == c or topo.may_write(c, d)]
         cross = [d for d in cores if d not in group]
         q = group.index(c)
-        direct = group[q + 1:] + group[:q]
+        ring = group[q + 1:] + group[:q]
+        direct = ring[:ND]
+        rot = q % len(cross)
+        rest = ring[ND:] + cross[rot:] + cross[:rot]
         here = [h for h in range(NSIM) if h not in cores
                 and topo.host(h) == topo.host(c) and topo.chip(h) == topo.chip(c)]
-        owners = [h for h in here if all(topo.may_write(h, d) for d in cross)]
-        dies = sorted(set(topo.die(h) for h in owners), key=lambda v: v != topo.die(c))
-        relays = [[h for h in owners if topo.die(h) == v][0] for v in dies][:NRELAY]
-        k = len(relays)
-        shares = []
-        for j in range(k):
-            part = [cross[p] for p in range(len(cross)) if (p + q) % k == j]
-            rot = (q // k) % len(part)
-            shares.append(part[rot:] + part[:rot])
-        plan[c] = {"direct": direct, "relays": relays, "shares": shares}
+        owners = [h for h in here if all(topo.may_write(h, d) for d in cores)]
+        far = [h for h in owners if topo.die(h) != topo.die(c)]
+        near = [h for h in owners if topo.die(h) == topo.die(c)]
+        helpers = (far + near)[:NH]
+        shares = [rest[j::len(helpers)] for j in range(len(helpers))]
+        m_out = _take(_common_mask(topo, c, direct), ENG)
+        m_chip = _common_mask(topo, c, helpers)
+        m_feed = _take(m_chip & ~m_out, ENG)
+        if _count(m_feed) != ENG:
+            m_feed = _take(m_chip, ENG)
+        plan[c] = {"direct": direct, "helpers": helpers, "shares": shares, "m_out": m_out, "m_feed": m_feed,
+                   "m_help": [_take(_common_mask(topo, h, sh), ENG) for h, sh in zip(helpers, shares)]}
     return plan
 
 
@@ -78,13 +92,6 @@ def _fused(g, topo, core, dsts, mask, sem, src, dst, local_sem):
                                           srcs=[src], dsts=[dst for _ in dsts], alu_op=0)], local_sem=local_sem)
 
 
-def _common_mask(topo, core, dsts):
-    m = topo.mask(core, dsts[0])
-    for d in dsts:
-        m &= topo.mask(core, d)
-    return m
-
-
 def rank_program(g, core, T, topo):
     S = T.sem
     plan = _plan(T, topo)
@@ -92,98 +99,112 @@ def rank_program(g, core, T, topo):
     rank = T.rank_of(core)
     Act = ActivationFunctionType
 
+    def xslot(s):
+        return T.land[:, s * C:(s + 1) * C]
+
+    def qslot(s):
+        return T.ql[:, s * QP:s * QP + 1]
+
     if rank is None:
         for c in cores:
-            if core in plan[c]["relays"]:
+            if core in plan[c]["helpers"]:
                 s = T.rank_of(c)
-                dsts = plan[c]["shares"][plan[c]["relays"].index(core)]
-                n_in = _count(_take(_common_mask(topo, c, plan[c]["relays"] + plan[c]["direct"]), ENG_CHIP))
-                m = _take(_common_mask(topo, core, dsts), ENG_OUT)
-                g.wait_ge(S.h, 2 * n_in)
-                _fused(g, topo, core, dsts, m, S["a%d" % s], T.msg[:], T.land[:, s * W:(s + 1) * W], S.loc)
-                g.wait_ge(S.loc, _count(m))
+                j = plan[c]["helpers"].index(core)
+                dsts, m = plan[c]["shares"][j], plan[c]["m_help"][j]
+                n_in = _count(plan[c]["m_feed"])
+                g.wait_ge(S.hx, n_in)
+                _fused(g, topo, core, dsts, m, S["ax%d" % s], T.xm[:], xslot(s), S.loc)
+                g.wait_ge(S.hq, n_in)
+                _fused(g, topo, core, dsts, m, S["aq%d" % s], T.qm[:], qslot(s), S.loc)
+                g.wait_ge(S.loc, 2 * _count(m))
         return
 
     me = plan[core]
-    direct, relays = me["direct"], me["relays"]
-    m_chip = _take(_common_mask(topo, core, relays + direct), ENG_CHIP)
-    m_out = _take(_common_mask(topo, core, direct), ENG_OUT)
+    direct, helpers, m_out, m_feed = me["direct"], me["helpers"], me["m_out"], me["m_feed"]
 
-    early = [T.rank_of(c) for c in cores if core in plan[c]["direct"]]
-    late = []
-    for c in cores:
-        for relay, share in zip(plan[c]["relays"], plan[c]["shares"]):
-            if core in share:
-                late.append((share.index(core), T.rank_of(c), _count(_take(_common_mask(topo, relay, share), ENG_OUT))))
-    late.sort()
-    n_early = 0
+    early, late = [], []
     for c in cores:
         if core in plan[c]["direct"]:
-            n_early += _count(_take(_common_mask(topo, c, plan[c]["direct"]), ENG_OUT))
+            early.append((plan[c]["direct"].index(core), 0, T.rank_of(c), _count(plan[c]["m_out"])))
+        for j, share in enumerate(plan[c]["shares"]):
+            if core in share:
+                late.append((share.index(core), j, T.rank_of(c), _count(plan[c]["m_help"][j])))
+    early = [(s, n) for _, _, s, n in sorted(early)]
+    late = [(s, n) for _, _, s, n in sorted(late)]
+    ne = len(early)
 
-    x = T.msg[:, 0:C]
-    q = T.msg[:, C:W]
+    x = T.xm[:]
+    H = slice(0, C)
+
+    def col(t, i, k=1):
+        return t[H, i * C:(i + k) * C]
 
     g.sync.dma_start(x, T.x[:]).then_inc(S.ld, 16)
     g.vector.memset(T.ones[:], 1.0).then_inc(S.cst, 1)
-    g.vector.memset(T.yb[0:C, rank * C:(rank + 1) * C], 0.0).then_inc(S.cp, 1)
+    g.vector.memset(T.one1[:], 1.0).then_inc(S.cst, 1)
+    g.vector.memset(T.qm[C:128, :], 1.0).then_inc(S.cst, 1)
+    g.vector.memset(col(T.yb, rank), 0.0).then_inc(S.cp, 1)
+    g.wait_ge(S.cst, 3)
+    g.affine_select(T.ident[H, :], T.ones[H, :], [[-1, C]], AluOpType.is_equal, 0.0, 0, 1).then_inc(S.idn, 1)
 
     g.wait_ge(S.ld, 16)
-    _fused(g, topo, core, relays, m_chip, S.h, x, x, S.loc)
+    _fused(g, topo, core, helpers, m_feed, S.hx, x, x, S.loc)
+    _fused(g, topo, core, direct, m_out, S["ax%d" % rank], x, xslot(rank), S.loc)
 
     g.scalar.wait_ge(S.ld, 16)
     g.scalar.activation(T.sq[:], x, Act.Square).then_inc(S.c1, 1)
-    g.tensor.wait_ge(S.cst, 1)
+    g.tensor.wait_ge(S.cst, 3)
     g.tensor.wait_ge(S.c1, 1)
-    g.tensor.matmul(T.ps0[:, 0:C], T.ones[:], T.sq[:], True, True).then_inc(S.c2, 1)
+    g.tensor.matmul(T.ps0[H, 0:1], T.sq[:], T.one1[:], True, True).then_inc(S.c2, 1)
     g.vector.wait_ge(S.c2, 1)
-    g.vector.reciprocal(T.rs[:], T.ps0[:, 0:C]).then_inc(S.c3, 1)
-    g.vector.wait_ge(S.c3, 1)
-    g.vector.tensor_copy(q, T.rs[:]).then_inc(S.c4, 1)
+    g.vector.reciprocal(T.qm[H, :], T.ps0[H, 0:1]).then_inc(S.c3, 1)
 
-    g.wait_ge(S.c4, 1)
-    _fused(g, topo, core, relays, m_chip, S.h, q, q, S.loc)
-    _fused(g, topo, core, direct, m_out, S.ae, T.msg[:], T.land[:, rank * W:(rank + 1) * W], S.loc)
+    g.wait_ge(S.c3, 1)
+    _fused(g, topo, core, helpers, m_feed, S.hq, T.qm[:], T.qm[:], S.loc)
+    _fused(g, topo, core, direct, m_out, S["aq%d" % rank], T.qm[:], qslot(rank), S.loc)
 
     g.scalar.wait_ge(S.c3, 1)
-    g.scalar.activation(T.inv[:], T.rs[:], Act.Sqrt).then_inc(S.c6, 1)
+    g.scalar.activation(T.ivc[H, :], T.qm[H, :], Act.Sqrt).then_inc(S.c6, 1)
+    g.scalar.wait_ge(S.idn, 1)
+
+    bank = [T["ps%d" % (2 + i)] for i in range(len(late))]
+
+    g.tensor.wait_ge(S.ld, 16)
+    g.tensor.wait_ge(S.c3, 1)
+    for i, (s, n) in enumerate(early):
+        g.tensor.wait_ge(S["ax%d" % s], n)
+        g.tensor.matmul(col(T.ps0, i), x, xslot(s), True, True).then_inc(S.e0, 1)
     g.vector.wait_ge(S.c6, 1)
-    g.vector.tensor_tensor(T.u[:], x, T.inv[:], AluOpType.mult).then_inc(S.c5, 1)
+    g.vector.wait_ge(S.e0, ne)
+    g.vector.tensor_scalar(col(T.gs, 0, ne), col(T.ps0, 0, ne), T.ivc[H, :], None, AluOpType.mult).then_inc(S.eg, 1)
+    for i, (s, n) in enumerate(late):
+        g.tensor.wait_ge(S["ax%d" % s], n)
+        g.tensor.matmul(col(bank[i], 0), x, xslot(s), True, True).then_inc(S["mg%d" % s], 1)
+        g.vector.wait_ge(S["mg%d" % s], 1)
+        g.vector.tensor_scalar(col(T.gs, ne + i), col(bank[i], 0), T.ivc[H, :], None,
+                               AluOpType.mult).then_inc(S["cg%d" % s], 1)
 
-    banks = ["ps%d" % b for b in range(1, NBANK)]
-    late_bank = banks[:len(late)]
-    early_bank = banks[len(late)]
+    for i, (s, n) in enumerate(early + late):
+        g.scalar.wait_ge(S["aq%d" % s], n)
+        g.scalar.activation(col(T.dg, i), T.ident[H, :], Act.Sqrt, scale=T.ql[H, s * QP:s * QP + 1]).then_inc(
+            S["dd%d" % s], 1)
 
-    def xs(s):
-        return T.land[:, s * W:s * W + C]
-
-    def qs(s):
-        return T.land[0:C, s * W + C:(s + 1) * W]
-
-    def blk(t, s):
-        return t[0:C, s * C:(s + 1) * C]
-
-    g.tensor.wait_ge(S.c5, 1)
-    g.tensor.wait_ge(S.ae, n_early)
-    g.scalar.wait_ge(S.ae, n_early)
-    for i, s in enumerate(early):
-        g.tensor.matmul(blk(T[early_bank], i), T.u[:], xs(s), True, True).then_inc(S.e0, 1)
-        g.scalar.activation(blk(T.iv, s), qs(s), Act.Sqrt).then_inc(S.ev, 1)
-    g.vector.wait_ge(S.e0, len(early))
-    g.vector.wait_ge(S.ev, len(early))
-    for i, s in enumerate(early):
-        g.vector.tensor_tensor(blk(T.yb, s), blk(T[early_bank], i), blk(T.iv, s), AluOpType.mult).then_inc(S.cp, 1)
-
-    for i, (pos, s, n) in enumerate(late):
-        g.tensor.wait_ge(S["a%d" % s], n)
-        g.tensor.matmul(T[late_bank[i]][0:C, 0:C], T.u[:], xs(s), True, True).then_inc(S["m%d" % s], 1)
-        g.scalar.wait_ge(S["a%d" % s], n)
-        g.scalar.activation(blk(T.iv, s), qs(s), Act.Sqrt).then_inc(S["v%d" % s], 1)
-        g.vector.wait_ge(S["m%d" % s], 1)
-        g.vector.wait_ge(S["v%d" % s], 1)
-        g.vector.tensor_tensor(blk(T.yb, s), T[late_bank[i]][0:C, 0:C], blk(T.iv, s), AluOpType.mult).then_inc(S.cp, 1)
+    for s, n in early:
+        g.tensor.wait_ge(S["dd%d" % s], 1)
+    g.tensor.matmul(col(T.ps1, 0, ne), T.ones[H, :], col(T.dg, 0, ne), True, True).then_inc(S.er, 1)
+    g.vector.wait_ge(S.er, 1)
+    g.vector.wait_ge(S.eg, 1)
+    for i, (s, n) in enumerate(early):
+        g.vector.tensor_tensor(col(T.yb, s), col(T.gs, i), col(T.ps1, i), AluOpType.mult).then_inc(S.cp, 1)
+    for i, (s, n) in enumerate(late):
+        g.tensor.wait_ge(S["dd%d" % s], 1)
+        g.tensor.wait_ge(S["cg%d" % s], 1)
+        g.tensor.matmul(col(bank[i], 1), T.ones[H, :], col(T.dg, ne + i), True, True).then_inc(S["rr%d" % s], 1)
+        g.vector.wait_ge(S["rr%d" % s], 1)
+        g.vector.wait_ge(S["cg%d" % s], 1)
+        g.vector.tensor_tensor(col(T.yb, s), col(T.gs, ne + i), col(bank[i], 1), AluOpType.mult).then_inc(S.cp, 1)
 
     g.sync.wait_ge(S.cp, NR)
-    g.sync.dma_start(T.y[:], T.yb[0:C, :]).then_inc(S.st, 16)
+    g.sync.dma_start(T.y[:], T.yb[H, :]).then_inc(S.st, 16)
     g.sync.wait_ge(S.st, 16)
-    g.wait_ge(S.loc, 2 * _count(m_chip) + _count(m_out))
+    g.wait_ge(S.loc, 2 * _count(m_feed) + 2 * _count(m_out))

@@ -22,11 +22,13 @@ SCRATCH = {
     "dg": ("sbuf", [128, NR * C], "bfloat16"),
     "gs": ("sbuf", [128, NR * C], "float32"),
     "yb": ("sbuf", [128, NR * C], "bfloat16"),
+    "zr": ("sbuf", [128, C], "bfloat16"),
 }
 for _b in range(8):
     SCRATCH["ps%d" % _b] = ("psum", [128, 512], "float32")
 
-SEMAPHORES = (["ld", "cst", "idn", "c1", "c2", "c3", "c6", "hx", "hq", "e0", "eg", "er", "cp", "loc", "st"]
+SEMAPHORES = (["ld", "cst", "idn", "c1", "c2", "c3", "c6", "hx", "hq", "e0", "eg", "er", "cp", "loc", "st",
+               "kid", "kon", "kz"]
               + [p + "%d" % _s for _s in range(NR) for p in ("ax", "aq", "mg", "cg", "dd", "rr")])
 
 
@@ -79,7 +81,7 @@ def _plan(T, topo):
         if _count(m_feed) != ENG:
             m_feed = _take(m_chip, ENG)
         plan[c] = {"direct": direct, "helpers": helpers, "shares": shares, "m_out": m_out, "m_feed": m_feed,
-                   "m_help": [_take(_common_mask(topo, h, sh), ENG) for h, sh in zip(helpers, shares)]}
+                   "m_help": [_take(_common_mask(topo, h, sh + [c]), ENG) for h, sh in zip(helpers, shares)]}
     return plan
 
 
@@ -112,15 +114,30 @@ def rank_program(g, core, T, topo):
                 j = plan[c]["helpers"].index(core)
                 dsts, m = plan[c]["shares"][j], plan[c]["m_help"][j]
                 n_in = _count(plan[c]["m_feed"])
+                if j == 0:
+                    g.vector.memset(T.ones[:], 1.0).then_inc(S.cst, 1)
+                    g.wait_ge(S.cst, 1)
+                    g.affine_select(T.ident[:], T.ones[:], [[-1, C]], AluOpType.is_equal, 0.0, 0, 1).then_inc(S.idn, 1)
+                    g.wait_ge(S.idn, 1)
+                    _fused(g, topo, core, [c], m, S.kid, T.ident[:], T.ident[:], S.loc)
+                elif j == 1:
+                    g.vector.memset(T.ones[:], 1.0).then_inc(S.cst, 1)
+                    g.wait_ge(S.cst, 1)
+                    _fused(g, topo, core, [c], m, S.kon, T.ones[:], T.ones[:], S.loc)
+                else:
+                    g.vector.memset(T.zr[:], 0.0).then_inc(S.cst, 1)
+                    g.wait_ge(S.cst, 1)
+                    _fused(g, topo, core, [c], m, S.kz, T.zr[:], T.yb[:, s * C:(s + 1) * C], S.loc)
                 g.wait_ge(S.hx, n_in)
                 _fused(g, topo, core, dsts, m, S["ax%d" % s], T.xm[:], xslot(s), S.loc)
                 g.wait_ge(S.hq, n_in)
                 _fused(g, topo, core, dsts, m, S["aq%d" % s], T.qm[:], qslot(s), S.loc)
-                g.wait_ge(S.loc, 2 * _count(m))
+                g.wait_ge(S.loc, 3 * _count(m))
         return
 
     me = plan[core]
     direct, helpers, m_out, m_feed = me["direct"], me["helpers"], me["m_out"], me["m_feed"]
+    nk = [_count(m) for m in me["m_help"]]
 
     early, late = [], []
     for c in cores:
@@ -140,12 +157,8 @@ def rank_program(g, core, T, topo):
         return t[H, i * C:(i + k) * C]
 
     g.sync.dma_start(x, T.x[:]).then_inc(S.ld, 16)
-    g.vector.memset(T.ones[:], 1.0).then_inc(S.cst, 1)
     g.vector.memset(T.one1[:], 1.0).then_inc(S.cst, 1)
     g.vector.memset(T.qm[C:128, :], 1.0).then_inc(S.cst, 1)
-    g.vector.memset(col(T.yb, rank), 0.0).then_inc(S.cp, 1)
-    g.wait_ge(S.cst, 3)
-    g.affine_select(T.ident[H, :], T.ones[H, :], [[-1, C]], AluOpType.is_equal, 0.0, 0, 1).then_inc(S.idn, 1)
 
     g.wait_ge(S.ld, 16)
     _fused(g, topo, core, helpers, m_feed, S.hx, x, x, S.loc)
@@ -153,19 +166,20 @@ def rank_program(g, core, T, topo):
 
     g.scalar.wait_ge(S.ld, 16)
     g.scalar.activation(T.sq[:], x, Act.Square).then_inc(S.c1, 1)
-    g.tensor.wait_ge(S.cst, 3)
+    g.tensor.wait_ge(S.cst, 2)
     g.tensor.wait_ge(S.c1, 1)
     g.tensor.matmul(T.ps0[H, 0:1], T.sq[:], T.one1[:], True, True).then_inc(S.c2, 1)
     g.vector.wait_ge(S.c2, 1)
     g.vector.reciprocal(T.qm[H, :], T.ps0[H, 0:1]).then_inc(S.c3, 1)
 
+    g.wait_ge(S.cst, 2)
     g.wait_ge(S.c3, 1)
     _fused(g, topo, core, helpers, m_feed, S.hq, T.qm[:], T.qm[:], S.loc)
     _fused(g, topo, core, direct, m_out, S["aq%d" % rank], T.qm[:], qslot(rank), S.loc)
 
     g.scalar.wait_ge(S.c3, 1)
     g.scalar.activation(T.ivc[H, :], T.qm[H, :], Act.Sqrt).then_inc(S.c6, 1)
-    g.scalar.wait_ge(S.idn, 1)
+    g.scalar.wait_ge(S.kid, nk[0])
 
     bank = [T["ps%d" % (2 + i)] for i in range(len(late))]
 
@@ -189,6 +203,7 @@ def rank_program(g, core, T, topo):
         g.scalar.activation(col(T.dg, i), T.ident[H, :], Act.Sqrt, scale=T.ql[H, s * QP:s * QP + 1]).then_inc(
             S["dd%d" % s], 1)
 
+    g.tensor.wait_ge(S.kon, nk[1])
     for s, n in early:
         g.tensor.wait_ge(S["dd%d" % s], 1)
     g.tensor.matmul(col(T.ps1, 0, ne), T.ones[H, :], col(T.dg, 0, ne), True, True).then_inc(S.er, 1)
@@ -204,7 +219,8 @@ def rank_program(g, core, T, topo):
         g.vector.wait_ge(S["cg%d" % s], 1)
         g.vector.tensor_tensor(col(T.yb, s), col(T.gs, ne + i), col(bank[i], 1), AluOpType.mult).then_inc(S.cp, 1)
 
-    g.sync.wait_ge(S.cp, NR)
+    g.sync.wait_ge(S.kz, nk[2])
+    g.sync.wait_ge(S.cp, NR - 1)
     g.sync.dma_start(T.y[:], T.yb[H, :]).then_inc(S.st, 16)
     g.sync.wait_ge(S.st, 16)
     g.wait_ge(S.loc, 2 * _count(m_feed) + 2 * _count(m_out))

from concourse.bass import DstId, RemoteDMATransfer
from concourse.mybir import AluOpType, ActivationFunctionType

NSIM = 256
C = 64
NR = 10
QP = 4
ND = 3
NH = 3
ENG = 8

SCRATCH = {
    "xm": ("sbuf", [128, C], "bfloat16"),
    "qm": ("sbuf", [128, 1], "float32"),
    "sq": ("sbuf", [128, C], "bfloat16"),
    "one1": ("sbuf", [128, 1], "bfloat16"),
    "ones": ("sbuf", [128, C], "bfloat16"),
    "ident": ("sbuf", [128, C], "bfloat16"),
    "ivc": ("sbuf", [128, 1], "float32"),
    "land": ("sbuf", [128, NR * C], "bfloat16"),
    "ql": ("sbuf", [128, NR * QP], "float32"),
    "dg": ("sbuf", [128, NR * C], "bfloat16"),
    "gs": ("sbuf", [128, NR * C], "float32"),
    "yb": ("sbuf", [128, NR * C], "bfloat16"),
    "zr": ("sbuf", [128, C], "bfloat16"),
}
for _b in range(8):
    SCRATCH["ps%d" % _b] = ("psum", [128, 512], "float32")

SEMAPHORES = (["ld", "cst", "idn", "c1", "c2", "c3", "c6", "hx", "hq", "e0", "eg", "er", "cp", "loc", "st",
               "kid", "kon", "kz"]
              + [p + "%d" % _s for _s in range(NR) for p in ("ax", "aq", "mg", "cg", "dd", "rr")])


def _take(mask, n):
    out, bit = 0, 1
    while n > 0 and bit <= mask:
        if mask & bit:
            out |= bit
            n -= 1
        bit <<= 1
    return out


def _count(mask):
    n = 0
    while mask:
        n += mask & 1
        mask >>= 1
    return n


def _common_mask(topo, core, dsts):
    m = topo.mask(core, dsts[0])
    for d in dsts:
        m &= topo.mask(core, d)
    return m


def _plan(T, topo):
    cores = list(T.cores)
    plan = {}
    for c in cores:
        group = [d for d in cores if d == c or topo.may_write(c, d)]
        cross = [d for d in cores if d not in group]
        q = group.index(c)
        ring = group[q + 1:] + group[:q]
        direct = ring[:ND]
        rot = q % len(cross)
        rest = ring[ND:] + cross[rot:] + cross[:rot]
        here = [h for h in range(NSIM) if h not in cores
                and topo.host(h) == topo.host(c) and topo.chip(h) == topo.chip(c)]
        owners = [h for h in here if all(topo.may_write(h, d) for d in cores)]
        far = [h for h in owners if topo.die(h) != topo.die(c)]
        near = [h for h in owners if topo.die(h) == topo.die(c)]
        helpers = (far + near)[:NH]
        shares = [rest[j::len(helpers)] for j in range(len(helpers))]
        m_out = _take(_common_mask(topo, c, direct), ENG)
        m_chip = _common_mask(topo, c, helpers)
        m_feed = _take(m_chip & ~m_out, ENG)
        if _count(m_feed) != ENG:
            m_feed = _take(m_chip, ENG)
        plan[c] = {"direct": direct, "helpers": helpers, "shares": shares, "m_out": m_out, "m_feed": m_feed,
                   "m_help": [_take(_common_mask(topo, h, sh + [c]), ENG) for h, sh in zip(helpers, shares)]}
    return plan


def _fused(g, topo, core, dsts, mask, sem, src, dst, local_sem):
    ids = []
    for d in dsts:
        rid, pid = topo.addr(d, core)
        ids.append(DstId(rid=rid, pnc=pid))
    g.remote_dma_fused([RemoteDMATransfer(dst_ids=ids, dma_engine_mask=mask, remote_sem=sem,
                                          srcs=[src], dsts=[dst for _ in dsts], alu_op=0)], local_sem=local_sem)


def rank_program(g, core, T, topo):
    S = T.sem
    plan = _plan(T, topo)
    cores = list(T.cores)
    rank = T.rank_of(core)
    Act = ActivationFunctionType

    def xslot(s):
        return T.land[:, s * C:(s + 1) * C]

    def qslot(s):
        return T.ql[:, s * QP:s * QP + 1]

    if rank is None:
        for c in cores:
            if core in plan[c]["helpers"]:
                s = T.rank_of(c)
                j = plan[c]["helpers"].index(core)
                dsts, m = plan[c]["shares"][j], plan[c]["m_help"][j]
                n_in = _count(plan[c]["m_feed"])
                if j == 0:
                    g.vector.memset(T.ones[:], 1.0).then_inc(S.cst, 1)
                    g.wait_ge(S.cst, 1)
                    g.affine_select(T.ident[:], T.ones[:], [[-1, C]], AluOpType.is_equal, 0.0, 0, 1).then_inc(S.idn, 1)
                    g.wait_ge(S.idn, 1)
                    _fused(g, topo, core, [c], m, S.kid, T.ident[:], T.ident[:], S.loc)
                elif j == 1:
                    g.vector.memset(T.ones[:], 1.0).then_inc(S.cst, 1)
                    g.wait_ge(S.cst, 1)
                    _fused(g, topo, core, [c], m, S.kon, T.ones[:], T.ones[:], S.loc)
                else:
                    g.vector.memset(T.zr[:], 0.0).then_inc(S.cst, 1)
                    g.wait_ge(S.cst, 1)
                    _fused(g, topo, core, [c], m, S.kz, T.zr[:], T.yb[:, s * C:(s + 1) * C], S.loc)
                g.wait_ge(S.hx, n_in)
                _fused(g, topo, core, dsts, m, S["ax%d" % s], T.xm[:], xslot(s), S.loc)
                g.wait_ge(S.hq, n_in)
                _fused(g, topo, core, dsts, m, S["aq%d" % s], T.qm[:], qslot(s), S.loc)
                g.wait_ge(S.loc, 3 * _count(m))
        return

    me = plan[core]
    direct, helpers, m_out, m_feed = me["direct"], me["helpers"], me["m_out"], me["m_feed"]
    nk = [_count(m) for m in me["m_help"]]

    early, late = [], []
    for c in cores:
        if core in plan[c]["direct"]:
            early.append((plan[c]["direct"].index(core), 0, T.rank_of(c), _count(plan[c]["m_out"])))
        for j, share in enumerate(plan[c]["shares"]):
            if core in share:
                late.append((share.index(core), j, T.rank_of(c), _count(plan[c]["m_help"][j])))
    early = [(s, n) for _, _, s, n in sorted(early)]
    late = [(s, n) for _, _, s, n in sorted(late)]
    ne = len(early)

    x = T.xm[:]
    H = slice(0, C)

    def col(t, i, k=1):
        return t[H, i * C:(i + k) * C]

    g.sync.dma_start(x, T.x[:]).then_inc(S.ld, 16)
    g.vector.memset(T.one1[:], 1.0).then_inc(S.cst, 1)
    g.vector.memset(T.qm[C:128, :], 1.0).then_inc(S.cst, 1)

    g.wait_ge(S.ld, 16)
    _fused(g, topo, core, helpers, m_feed, S.hx, x, x, S.loc)
    _fused(g, topo, core, direct, m_out, S["ax%d" % rank], x, xslot(rank), S.loc)

    g.scalar.wait_ge(S.ld, 16)
    g.scalar.activation(T.sq[:], x, Act.Square).then_inc(S.c1, 1)
    g.tensor.wait_ge(S.cst, 2)
    g.tensor.wait_ge(S.c1, 1)
    g.tensor.matmul(T.ps0[H, 0:1], T.sq[:], T.one1[:], True, True).then_inc(S.c2, 1)
    g.vector.wait_ge(S.c2, 1)
    g.vector.reciprocal(T.qm[H, :], T.ps0[H, 0:1]).then_inc(S.c3, 1)

    g.wait_ge(S.cst, 2)
    g.wait_ge(S.c3, 1)
    _fused(g, topo, core, helpers, m_feed, S.hq, T.qm[:], T.qm[:], S.loc)
    _fused(g, topo, core, direct, m_out, S["aq%d" % rank], T.qm[:], qslot(rank), S.loc)

    g.scalar.wait_ge(S.c3, 1)
    g.scalar.activation(T.ivc[H, :], T.qm[H, :], Act.Sqrt).then_inc(S.c6, 1)
    g.scalar.wait_ge(S.kid, nk[0])

    bank = [T["ps%d" % (2 + i)] for i in range(len(late))]

    g.tensor.wait_ge(S.ld, 16)
    g.tensor.wait_ge(S.c3, 1)
    for i, (s, n) in enumerate(early):
        g.tensor.wait_ge(S["ax%d" % s], n)
        g.tensor.matmul(col(T.ps0, i), x, xslot(s), True, True).then_inc(S.e0, 1)
    g.vector.wait_ge(S.c6, 1)
    g.vector.wait_ge(S.e0, ne)
    g.vector.tensor_scalar(col(T.gs, 0, ne), col(T.ps0, 0, ne), T.ivc[H, :], None, AluOpType.mult).then_inc(S.eg, 1)
    for i, (s, n) in enumerate(late):
        g.tensor.wait_ge(S["ax%d" % s], n)
        g.tensor.matmul(col(bank[i], 0), x, xslot(s), True, True).then_inc(S["mg%d" % s], 1)
        g.vector.wait_ge(S["mg%d" % s], 1)
        g.vector.tensor_scalar(col(T.gs, ne + i), col(bank[i], 0), T.ivc[H, :], None,
                               AluOpType.mult).then_inc(S["cg%d" % s], 1)

    for i, (s, n) in enumerate(early + late):
        g.scalar.wait_ge(S["aq%d" % s], n)
        g.scalar.activation(col(T.dg, i), T.ident[H, :], Act.Sqrt, scale=T.ql[H, s * QP:s * QP + 1]).then_inc(
            S["dd%d" % s], 1)

    g.tensor.wait_ge(S.kon, nk[1])
    for s, n in early:
        g.tensor.wait_ge(S["dd%d" % s], 1)
    g.tensor.matmul(col(T.ps1, 0, ne), T.ones[H, :], col(T.dg, 0, ne), True, True).then_inc(S.er, 1)
    g.vector.wait_ge(S.er, 1)
    g.vector.wait_ge(S.eg, 1)
    for i, (s, n) in enumerate(early):
        g.vector.tensor_tensor(col(T.yb, s), col(T.gs, i), col(T.ps1, i), AluOpType.mult).then_inc(S.cp, 1)
    for i, (s, n) in enumerate(late):
        g.tensor.wait_ge(S["dd%d" % s], 1)
        g.tensor.wait_ge(S["cg%d" % s], 1)
        g.tensor.matmul(col(bank[i], 1), T.ones[H, :], col(T.dg, ne + i), True, True).then_inc(S["rr%d" % s], 1)
        g.vector.wait_ge(S["rr%d" % s], 1)
        g.vector.wait_ge(S["cg%d" % s], 1)
        g.vector.tensor_tensor(col(T.yb, s), col(T.gs, ne + i), col(bank[i], 1), AluOpType.mult).then_inc(S.cp, 1)

    g.sync.wait_ge(S.kz, nk[2])
    g.sync.wait_ge(S.cp, NR - 1)
    g.sync.dma_start(T.y[:], T.yb[H, :]).then_inc(S.st, 16)
    g.sync.wait_ge(S.st, 16)
    g.wait_ge(S.loc, 2 * _count(m_feed) + 2 * _count(m_out))
